import numpy as np
import ml_dtypes


def mxq(x, axis, fmt="e4m3"):
    dtype, down = {"e4m3": (ml_dtypes.float8_e4m3fn, 7), "e5m2": (ml_dtypes.float8_e5m2, 14)}[fmt]
    v = np.moveaxis(np.asarray(x, np.float32).astype(ml_dtypes.bfloat16).astype(np.float64), axis, -1)
    blocks = v.reshape(v.shape[:-1] + (-1, 32))
    amax = np.abs(blocks).max(-1, keepdims=True)
    byte = np.maximum(np.where(amax > 0, np.frexp(amax)[1] - 1 + 127, 0) - down, 1)
    scale = np.exp2(byte - 127.0)
    codes = (blocks / scale).astype(np.float32).astype(dtype).astype(np.float64)
    return np.moveaxis((codes * scale).reshape(v.shape), -1, axis)


WIDE = False


def mx_kscale(k):
    if not WIDE:
        return np.ones(k)
    levels = np.array([10, -10, 5, -5, 0])
    if k % 512:
        return np.exp2(np.random.permutation(np.resize(levels, k // 32))).repeat(32)
    a = np.empty((k // 512, 16))
    for p in range(k // 512):
        a[p, :8] = np.random.permutation(np.resize(levels, 8))
        for g in range(8):
            far = levels[np.abs(levels - a[p, g]) >= 10]
            a[p, g + 8] = far[np.random.randint(len(far))]
    return np.exp2(a.ravel()).repeat(32)


def f64(x):
    return np.asarray(x).astype(np.float64)


def striped(idx):
    return np.tile(idx.reshape(-1, 16).T, (8, 1)).astype(np.uint16)


def unstriped(offs):
    return offs[:16].T.reshape(-1).astype(np.int64)


E2M1 = np.array([0.0, 0.5, 1.0, 1.5, 2.0, 3.0, 4.0, 6.0, -0.0, -0.5, -1.0, -1.5, -2.0, -3.0, -4.0, -6.0])


def pack_weight(w, fmt):
    k, n = w.shape
    w = f64(np.asarray(w, np.float32).astype(ml_dtypes.bfloat16)).reshape(k // 32, 32, n)
    amax = np.abs(w).max(1)
    if fmt == "e4m3":
        byte = np.frexp(amax)[1] - 1 + 127 - 7
    else:
        mant, ex = np.frexp(amax / 6.0)
        byte = np.where(mant > 0.5, ex, ex - 1) + 127
    byte = np.clip(np.where(amax > 0, byte, 1), 1, 254)
    scaled = (w * np.exp2(127.0 - byte)[:, None, :]).reshape(k, n).astype(np.float32)
    by_word = np.ascontiguousarray(scaled.reshape(k // 512, 128, 4, n).transpose(0, 1, 3, 2))
    if fmt == "e4m3":
        words = by_word.astype(ml_dtypes.float8_e4m3fn).view(np.uint8)
    else:
        c = by_word.astype(ml_dtypes.float4_e2m1fn).view(np.uint8) & 0xF
        words = (c[..., 0::2] | (c[..., 1::2] << 4)).reshape(k // 512, 128, 2 * n)
    return np.ascontiguousarray(words), np.ascontiguousarray(byte.astype(np.uint8).reshape(k // 512, 16, n))


def unpack_weight(words, scales, fmt):
    g, _, n = scales.shape
    words = np.ascontiguousarray(words).reshape(g, 128, n, -1)
    if fmt == "e4m3":
        vals = words.view(ml_dtypes.float8_e4m3fn).astype(np.float64)
    else:
        nib = np.empty((g, 128, n, 4), np.uint8)
        nib[..., 0::2] = words & 0xF
        nib[..., 1::2] = words >> 4
        vals = E2M1[nib]
    vals = vals * np.repeat(np.exp2(scales.astype(np.float64) - 127.0), 8, axis=1)[..., None]
    return vals.transpose(0, 1, 3, 2).reshape(g * 512, n)


def gelu(v):
    return 0.5 * v * (1.0 + np.tanh(np.sqrt(2.0 / np.pi) * (v + 0.044715 * v**3)))


K, T, S, H, S2, T3, P = 1024, 4096, 1024, 512, 1024, 2048, 512

def setup_inputs():
    n = np.random.standard_normal
    s = mx_kscale(K)[:, None]
    u = mx_kscale(H)[:, None]
    tab_words, tab_scales = pack_weight(n((K, T)) * s, "e4m3")
    tab2_words, tab2_scales = pack_weight(n((H, T3)) / np.sqrt(H) / u, "e4m3")
    w4_words, w4_scales = pack_weight(n((K, H)) / np.sqrt(K) / s, "e2m1")
    return {
        "tab_words": tab_words, "tab_scales": tab_scales,
        "offs": striped(np.random.permutation(T)[:S]),
        "tab2_words": tab2_words, "tab2_scales": tab2_scales,
        "offs2": striped(np.random.permutation(T3)[:S2]),
        "pos1": striped(np.random.permutation(S)[:P]),
        "pos2": striped(np.random.permutation(S)[:P]),
        "w1": (n((K, H)) / np.sqrt(K) / s).astype(np.float32),
        "w2": (n((K, H)) / np.sqrt(K) / s).astype(np.float32),
        "w4_words": w4_words, "w4_scales": w4_scales,
        "gain": (np.exp(0.3 * n(H)) * u[:, 0]).astype(np.float32),
        "left": n((H, P)).astype(np.float32),
        "fit": n((S2, P)).astype(np.float32),
        "bias": (0.7 * n(S2)).astype(np.float32),
    }

def reference(tab_words, tab_scales, offs, tab2_words, tab2_scales, offs2, pos1, pos2,
              w1, w2, w4_words, w4_scales, gain, left, fit, bias):
    v = unpack_weight(tab_words, tab_scales, "e4m3")[:, unstriped(offs)]
    v2 = unpack_weight(tab2_words, tab2_scales, "e4m3")[:, unstriped(offs2)]
    w4 = unpack_weight(w4_words, w4_scales, "e2m1")
    b1 = mxq(f64(w1), 0, "e4m3").T @ v
    b2 = mxq(f64(w2), 0, "e4m3").T @ v
    b3 = w4.T @ v
    h = (np.maximum(b1, b2) + b3) * f64(gain)[:, None]
    x1 = mxq(h[:, unstriped(pos1)] * f64(left), 0, "e4m3")
    x2 = mxq(h[:, unstriped(pos2)], 0, "e4m3")
    e1 = v2.T @ x1
    e2 = v2.T @ x2
    return np.minimum(e1, e2) * f64(fit) + f64(bias)[:, None]

@@ -1,0 +1,268 @@
+from contextlib import ExitStack
+
+import concourse.mybir as mybir
+
+K, T, S, H, S2, T3, NP = 1024, 4096, 1024, 512, 1024, 2048, 512
+FLOPS = 2 * 3 * K * H * S + 2 * 2 * H * S2 * NP
+
+F32 = mybir.dt.float32
+BF16 = mybir.dt.bfloat16
+I32 = mybir.dt.int32
+U32 = mybir.dt.uint32
+U16 = mybir.dt.uint16
+U8 = mybir.dt.uint8
+FP8X4 = mybir.dt.float8_e4m3fn_x4
+FP4X4 = mybir.dt.float4_e2m1fn_x4
+ALU = mybir.AluOpType
+ACT = mybir.ActivationFunctionType
+
+P = 128
+PACK = 4
+PASSES = K // (P * PACK)
+BANK = 512
+HALVES = S // BANK
+M_TILES = S2 // P
+
+
+def tile_list_glove_pattern_chooser_kernel(
+    tc, tab_words, tab_scales, offs, tab2_words, tab2_scales, offs2, pos1, pos2,
+    w1, w2, w4_words, w4_scales, gain, left, fit, bias, out,
+):
+    nc = tc.nc
+    with ExitStack() as ctx:
+        keep = ctx.enter_context(tc.tile_pool(name="keep", bufs=1))
+        ring = ctx.enter_context(tc.tile_pool(name="ring", bufs=3))
+        psum = ctx.enter_context(tc.psum_pool(name="psum", bufs=1))
+
+        def held(shape, dtype, name, tag=None):
+            return keep.tile(shape, dtype, name=name, tag=tag or name, align_bytes=64)
+
+        offs_sb = held([P, S // 16], U16, "offs_sb")
+        offs2_sb = held([P, S2 // 16], U16, "offs2_sb")
+        pos1_sb = held([P, NP // 16], U16, "pos1_sb")
+        pos2_sb = held([P, NP // 16], U16, "pos2_sb")
+        tab_sc = held([P, T], U8, "tab_sc")
+        tab2_sc = held([P, T3], U8, "tab2_sc")
+        w4_sc_raw = held([P, PASSES, H], U8, "w4_sc_raw")
+        v_planes = [held([P, S], U8, "v_plane%d" % a) for a in range(PASSES)]
+        v2_plane = held([P, S2], U8, "v2_plane")
+
+        nc.vector.memset(tab_sc[:].bitcast(I32), 0)
+        nc.vector.memset(tab2_sc[:].bitcast(I32), 0)
+        nc.gpsimd.memset(w4_sc_raw[:].rearrange("p a c -> p (a c)").bitcast(I32), 0)
+
+        nc.sync.dma_start(offs_sb[:], offs)
+        nc.sync.dma_start(offs2_sb[:], offs2)
+        nc.scalar.dma_start(
+            out=tab_sc[0:P:4, :].bitcast(I32),
+            in_=tab_scales.rearrange("a q t -> (a q) t").bitcast(I32),
+        )
+        nc.scalar.dma_start(out=tab2_sc[0:P:8, :].bitcast(I32), in_=tab2_scales[0].bitcast(I32))
+        for q in range(4):
+            nc.gpsimd.dma_start(
+                out=w4_sc_raw[32 * q : 32 * q + 4, :, :].bitcast(I32),
+                in_=w4_scales[:, 4 * q : 4 * q + 4, :].rearrange("a r c -> r a c").bitcast(I32),
+            )
+        for plane in v_planes + [v2_plane]:
+            nc.gpsimd.memset(plane[:].bitcast(I32), 0)
+
+        w4_raw = held([P, PASSES, 2 * H], U8, "w4_raw")
+        nc.sync.dma_start(out=w4_raw[:].bitcast(I32), in_=w4_words.rearrange("a p b -> p a b").bitcast(I32))
+
+        def load_w(w, a, name, pieces):
+            rows = w[a * P * PACK : (a + 1) * P * PACK, :].rearrange("(p j) c -> p j c", j=PACK)
+            width = H // pieces
+            tiles = []
+            for i in range(pieces):
+                raw = held([P, PACK, width], F32, "%s_raw%d_%d" % (name, a, i))
+                nc.sync.dma_start(out=raw[:], in_=rows[:, :, i * width : (i + 1) * width])
+                tiles.append(raw)
+            return tiles
+
+        def load_words(words, a, width, name):
+            tile = held([P, width], U32, name)
+            nc.sync.dma_start(out=tile[:].bitcast(I32), in_=words[a].rearrange("p t i -> p (t i)").bitcast(I32))
+            return tile
+
+        w1_raw, tab_w = [], []
+        for a in range(PASSES):
+            w1_raw.append(load_w(w1, a, "w1", 1))
+            tab_w.append(load_words(tab_words, a, T, "tab_w%d" % a))
+        w2_raw = [load_w(w2, a, "w2", 2) for a in range(PASSES)]
+        nc.sync.dma_start(pos1_sb[:], pos1)
+        nc.sync.dma_start(pos2_sb[:], pos2)
+        gain_sb = held([P, PACK], F32, "gain_sb")
+        nc.sync.dma_start(out=gain_sb[:], in_=gain.rearrange("(p t) -> p t", t=PACK))
+        left_sb = held([P, PACK, NP], F32, "left_sb")
+        nc.sync.dma_start(out=left_sb[:], in_=left.rearrange("(p t) n -> p t n", t=PACK))
+        tab2_w = load_words(tab2_words, 0, T3, "tab2_w")
+        fit_sb = held([P, M_TILES, NP], F32, "fit_sb")
+        nc.sync.dma_start(out=fit_sb[:], in_=fit.rearrange("(c p) n -> p c n", p=P))
+        bias_sb = held([P, M_TILES], F32, "bias_sb")
+        with nc.allow_non_contiguous_dma(reason="one bias value a partition"):
+            nc.sync.dma_start(out=bias_sb[:], in_=bias.rearrange("(c p) -> p c", p=P))
+
+        v_sc = held([P, S], U8, "v_sc")
+        nc.vector.tensor_copy(v_sc[:], tab_sc[:].indirect(offs_sb[:]))
+        for a in range(PASSES):
+            for q in range(4):
+                first = 4 * (16 * a + 4 * q)
+                nc.gpsimd.dma_start(
+                    out=v_planes[a][32 * q : 32 * q + 4, :].bitcast(I32),
+                    in_=v_sc[first : first + 16 : 4, :].bitcast(I32),
+                )
+
+        w4_codes = held([P, PASSES, 2 * H], U8, "w4_codes")
+        w4_sc = held([P, PASSES, H], U8, "w4_sc")
+        nc.vector.tensor_copy(
+            w4_codes[:].bitcast(U16).rearrange("p a (t m) -> p a m t", t=PACK),
+            w4_raw[:].bitcast(U16).rearrange("p a (m t) -> p a m t", t=PACK),
+        )
+        nc.vector.tensor_copy(
+            w4_sc[:].rearrange("p a (t m) -> p a m t", t=PACK),
+            w4_sc_raw[:].rearrange("p a (m t) -> p a m t", t=PACK),
+        )
+
+        v2_sc = held([P, S2], U8, "v2_sc")
+        nc.vector.tensor_copy(v2_sc[:], tab2_sc[:].indirect(offs2_sb[:]))
+        for q in range(4):
+            nc.gpsimd.dma_start(
+                out=v2_plane[32 * q : 32 * q + 4, :].bitcast(I32),
+                in_=v2_sc[32 * q : 32 * q + 32 : 8, :].bitcast(I32),
+            )
+
+        def round_piece(copy, grouped, raw, first_m):
+            count = raw.shape[2] // PACK
+            copy(
+                grouped[:, :, first_m : first_m + count, :].rearrange("p t m j -> p m j t"),
+                raw[:].rearrange("p j (m t) -> p m j t", t=PACK),
+            )
+
+        def quantise(grouped, codes, scales, t0, t1):
+            nc.vector.quantize_mx(
+                out=codes[:, t0 * P : t1 * P].bitcast(FP8X4),
+                scales=scales[:, t0 * P : t1 * P],
+                in_=grouped[:, t0:t1, :, :].rearrange("p t m j -> p (t m j)"),
+            )
+
+        def mx_tiles(name, width):
+            return held([P, width], U32, name + "_codes"), held([P, width], U8, name + "_scales")
+
+        v_w, w1_q, w2_q = [], [], []
+        for a in range(PASSES):
+            grouped = held([P, PACK, P, PACK], BF16, "w1_bf%d" % a)
+            round_piece(nc.scalar.copy, grouped, w1_raw[a][0], 0)
+            w1_q.append(mx_tiles("w1_%d" % a, H))
+            quantise(grouped, w1_q[a][0], w1_q[a][1], 0, PACK)
+            v_w.append(held([P, S], U32, "v_w%d" % a))
+            for hf in range(HALVES):
+                nc.vector.tensor_copy(
+                    v_w[a][:, hf * BANK : (hf + 1) * BANK],
+                    tab_w[a][:].indirect(offs_sb[:, hf * 32 : (hf + 1) * 32]),
+                )
+        for a in range(PASSES):
+            grouped = held([P, PACK, P, PACK], BF16, "w2_bf%d" % a)
+            round_piece(nc.scalar.copy, grouped, w2_raw[a][0], 0)
+            round_piece(nc.vector.tensor_copy, grouped, w2_raw[a][1], P // 2)
+            w2_q.append(mx_tiles("w2_%d" % a, H))
+            quantise(grouped, w2_q[a][0], w2_q[a][1], 0, 1)
+            quantise(grouped, w2_q[a][0], w2_q[a][1], 1, PACK)
+
+        def product(kind, t, hf):
+            cols = slice(hf * BANK, (hf + 1) * BANK)
+            rows = slice(t * P, (t + 1) * P)
+            acc = psum.tile([P, BANK], F32, name="acc_" + kind, tag=kind, bufs={"b1": 2, "b2": 3, "b3": 3}[kind])
+            for a in range(PASSES):
+                if kind == "b3":
+                    lhs = w4_codes[:, a, 2 * t * P : 2 * (t + 1) * P].bitcast(FP4X4)
+                    lhs_sc = w4_sc[:, a, rows]
+                else:
+                    codes, scales = (w1_q if kind == "b1" else w2_q)[a]
+                    lhs = codes[:, rows].bitcast(FP8X4)
+                    lhs_sc = scales[:, rows]
+                nc.tensor.matmul_mx(
+                    out=acc[:], lhsT=lhs, lhsT_scale=lhs_sc,
+                    rhs=v_w[a][:, cols].bitcast(FP8X4), rhs_scale=v_planes[a][:, cols],
+                    start=(a == 0), stop=(a == PASSES - 1),
+                )
+            return acc
+
+        u = [held([P, S], F32, "u%d" % t) for t in range(PACK)]
+        x1_bf = held([P, NP, PACK], BF16, "x1_bf", tag="w1_bf0")
+        x2_bf = held([P, NP, PACK], BF16, "x2_bf", tag="w1_bf1")
+        larger = {}
+
+        def maximum(t, hf):
+            b1 = product("b1", t, hf)
+            b1_sb = held([P, BANK], F32, "b1_sb%d_%d" % (t, hf))
+            nc.scalar.copy(b1_sb[:], b1[:])
+            b2 = product("b2", t, hf)
+            larger[t, hf] = ring.tile([P, BANK], F32, name="larger")
+            nc.vector.tensor_tensor(larger[t, hf][:], b2[:], b1_sb[:], ALU.max)
+
+        def join(t, hf):
+            b3 = product("b3", t, hf)
+            nc.vector.tensor_tensor(u[t][:, hf * BANK : (hf + 1) * BANK], b3[:], larger[t, hf][:], ALU.add)
+
+        def pick(t):
+            g2 = ring.tile([P, NP], F32, name="g2")
+            nc.vector.tensor_copy(g2[:], u[t][:].indirect(pos2_sb[:]))
+            nc.scalar.activation(x2_bf[:, :, t], g2[:], ACT.Copy, scale=gain_sb[:, t : t + 1])
+            g1 = ring.tile([P, NP], F32, name="g1")
+            nc.vector.tensor_tensor(g1[:], u[t][:].indirect(pos1_sb[:]), left_sb[:, t, :], ALU.mult)
+            nc.scalar.activation(x1_bf[:, :, t], g1[:], ACT.Copy, scale=gain_sb[:, t : t + 1])
+
+        for t in range(PACK):
+            maximum(t, 0)
+            if t > 0:
+                pick(t - 1)
+            maximum(t, 1)
+            join(t, 0)
+            join(t, 1)
+        pick(PACK - 1)
+
+        v2_w = held([P, S2], U32, "v2_w", tag="u%d" % (PACK - 1))
+        x_q = {}
+        for hf, (name, x_bf) in enumerate((("x2", x2_bf), ("x1", x1_bf))):
+            nc.vector.tensor_copy(
+                v2_w[:, hf * BANK : (hf + 1) * BANK],
+                tab2_w[:].indirect(offs2_sb[:, hf * 32 : (hf + 1) * 32]),
+            )
+            x_q[name] = mx_tiles(name, NP)
+            nc.vector.quantize_mx(
+                out=x_q[name][0][:].bitcast(FP8X4), scales=x_q[name][1][:],
+                in_=x_bf[:].rearrange("p n t -> p (n t)"),
+            )
+
+        def score(name, tag, i):
+            rows = slice(i * P, (i + 1) * P)
+            acc = psum.tile([P, NP], F32, name="e_" + name, tag=tag, bufs=3)
+            nc.tensor.matmul_mx(
+                out=acc[:], lhsT=v2_w[:, rows].bitcast(FP8X4), lhsT_scale=v2_plane[:, rows],
+                rhs=x_q[name][0][:].bitcast(FP8X4), rhs_scale=x_q[name][1][:],
+                start=True, stop=True,
+            )
+            return acc
+
+        smaller = {}
+
+        def minimum(i):
+            e2 = score("x2", "b3", i)
+            e2_sb = ring.tile([P, NP], F32, name="e2_sb")
+            nc.scalar.copy(e2_sb[:], e2[:])
+            e1 = score("x1", "b2", i)
+            smaller[i] = ring.tile([P, NP], F32, name="smaller")
+            nc.vector.tensor_tensor(smaller[i][:], e1[:], e2_sb[:], ALU.min)
+
+        def finish(i):
+            fitted = ring.tile([P, NP], F32, name="fitted")
+            nc.vector.tensor_tensor(fitted[:], smaller[i][:], fit_sb[:, i, :], ALU.mult)
+            result = ring.tile([P, NP], F32, name="result")
+            nc.scalar.activation(result[:], fitted[:], ACT.Identity, bias=bias_sb[:, i : i + 1])
+            nc.sync.dma_start(out=out[i * P : (i + 1) * P, :], in_=result[:])
+
+        for i in range(M_TILES):
+            minimum(i)
+            if i > 0:
+                finish(i - 1)
+        finish(M_TILES - 1)

@@ -31,11 +31,15 @@ def tile_list_glove_pattern_chooser_kernel(
     nc = tc.nc
     with ExitStack() as ctx:
         keep = ctx.enter_context(tc.tile_pool(name="keep", bufs=1))
+        stage = ctx.enter_context(tc.tile_pool(name="stage", bufs=1))
         ring = ctx.enter_context(tc.tile_pool(name="ring", bufs=3))
         psum = ctx.enter_context(tc.psum_pool(name="psum", bufs=1))
 
         def held(shape, dtype, name, tag=None):
             return keep.tile(shape, dtype, name=name, tag=tag or name, align_bytes=64)
+
+        def staged(shape, dtype, name, kib):
+            return stage.tile(shape, dtype, name=name, offset=kib * 1024)
 
         offs_sb = held([P, S // 16], U16, "offs_sb")
         offs2_sb = held([P, S2 // 16], U16, "offs2_sb")
@@ -47,69 +51,48 @@ def tile_list_glove_pattern_chooser_kernel(
         v_planes = [held([P, S], U8, "v_plane%d" % a) for a in range(PASSES)]
         v2_plane = held([P, S2], U8, "v2_plane")
 
-        nc.vector.memset(tab_sc[:].bitcast(I32), 0)
-        nc.vector.memset(tab2_sc[:].bitcast(I32), 0)
-        nc.gpsimd.memset(w4_sc_raw[:].rearrange("p a c -> p (a c)").bitcast(I32), 0)
-
-        nc.sync.dma_start(offs_sb[:], offs)
-        nc.sync.dma_start(offs2_sb[:], offs2)
-        nc.scalar.dma_start(
-            out=tab_sc[0:P:4, :].bitcast(I32),
-            in_=tab_scales.rearrange("a q t -> (a q) t").bitcast(I32),
-        )
-        nc.scalar.dma_start(out=tab2_sc[0:P:8, :].bitcast(I32), in_=tab2_scales[0].bitcast(I32))
-        for q in range(4):
-            nc.gpsimd.dma_start(
-                out=w4_sc_raw[32 * q : 32 * q + 4, :, :].bitcast(I32),
-                in_=w4_scales[:, 4 * q : 4 * q + 4, :].rearrange("a r c -> r a c").bitcast(I32),
-            )
+        nc.gpsimd.memset(tab2_sc[:].bitcast(I32), 0)
+        nc.vector.memset(tab_sc[32:64, :].bitcast(I32), 0)
+        nc.vector.memset(tab_sc[64:P, :].bitcast(I32), 0)
+        nc.vector.memset(w4_sc_raw[:].rearrange("p a c -> p (a c)").bitcast(I32), 0)
         for plane in v_planes + [v2_plane]:
             nc.gpsimd.memset(plane[:].bitcast(I32), 0)
 
-        w4_raw = held([P, PASSES, 2 * H], U8, "w4_raw")
-        nc.sync.dma_start(out=w4_raw[:].bitcast(I32), in_=w4_words.rearrange("a p b -> p a b").bitcast(I32))
-
-        def load_w(w, a, name, pieces):
-            rows = w[a * P * PACK : (a + 1) * P * PACK, :].rearrange("(p j) c -> p j c", j=PACK)
-            width = H // pieces
-            tiles = []
-            for i in range(pieces):
-                raw = held([P, PACK, width], F32, "%s_raw%d_%d" % (name, a, i))
-                nc.sync.dma_start(out=raw[:], in_=rows[:, :, i * width : (i + 1) * width])
-                tiles.append(raw)
-            return tiles
-
-        def load_words(words, a, width, name):
-            tile = held([P, width], U32, name)
+        def load_words(words, a, width, name, kib):
+            tile = staged([P, width], U32, name, kib)
             nc.sync.dma_start(out=tile[:].bitcast(I32), in_=words[a].rearrange("p t i -> p (t i)").bitcast(I32))
             return tile
 
-        w1_raw, tab_w = [], []
-        for a in range(PASSES):
-            w1_raw.append(load_w(w1, a, "w1", 1))
-            tab_w.append(load_words(tab_words, a, T, "tab_w%d" % a))
-        w2_raw = [load_w(w2, a, "w2", 2) for a in range(PASSES)]
+        nc.sync.dma_start(offs_sb[:], offs)
+        nc.sync.dma_start(
+            out=tab_sc[0:32, :].bitcast(I32),
+            in_=tab_scales.rearrange("a q t -> (a q) t").bitcast(I32),
+        )
+        nc.sync.dma_start(offs2_sb[:], offs2)
         nc.sync.dma_start(pos1_sb[:], pos1)
         nc.sync.dma_start(pos2_sb[:], pos2)
+        w4_raw = held([P, PASSES, 2 * H], U8, "w4_raw")
+        nc.sync.dma_start(out=w4_raw[:].bitcast(I32), in_=w4_words.rearrange("a p b -> p a b").bitcast(I32))
+        nc.sync.dma_start(out=tab2_sc[0:P:8, :].bitcast(I32), in_=tab2_scales[0].bitcast(I32))
+        w1_raw = staged([P, PASSES, PACK, H], F32, "w1_raw", 32)
+        nc.sync.dma_start(out=w1_raw[:], in_=w1.rearrange("(a p j) c -> p a j c", p=P, j=PACK))
+        for q in range(4):
+            nc.sync.dma_start(
+                out=w4_sc_raw[32 * q : 32 * q + 4, :, :].bitcast(I32),
+                in_=w4_scales[:, 4 * q : 4 * q + 4, :].rearrange("a r c -> r a c").bitcast(I32),
+            )
+        tab_w = [load_words(tab_words, a, T, "tab_w%d" % a, 16 * a) for a in range(PASSES)]
         gain_sb = held([P, PACK], F32, "gain_sb")
         nc.sync.dma_start(out=gain_sb[:], in_=gain.rearrange("(p t) -> p t", t=PACK))
-        left_sb = held([P, PACK, NP], F32, "left_sb")
-        nc.sync.dma_start(out=left_sb[:], in_=left.rearrange("(p t) n -> p t n", t=PACK))
-        tab2_w = load_words(tab2_words, 0, T3, "tab2_w")
-        fit_sb = held([P, M_TILES, NP], F32, "fit_sb")
-        nc.sync.dma_start(out=fit_sb[:], in_=fit.rearrange("(c p) n -> p c n", p=P))
-        bias_sb = held([P, M_TILES], F32, "bias_sb")
-        with nc.allow_non_contiguous_dma(reason="one bias value a partition"):
-            nc.sync.dma_start(out=bias_sb[:], in_=bias.rearrange("(c p) -> p c", p=P))
 
         v_sc = held([P, S], U8, "v_sc")
         nc.vector.tensor_copy(v_sc[:], tab_sc[:].indirect(offs_sb[:]))
         for a in range(PASSES):
             for q in range(4):
-                first = 4 * (16 * a + 4 * q)
-                nc.gpsimd.dma_start(
+                first = 16 * a + 4 * q
+                (nc.scalar if a == 0 else nc.gpsimd).dma_start(
                     out=v_planes[a][32 * q : 32 * q + 4, :].bitcast(I32),
-                    in_=v_sc[first : first + 16 : 4, :].bitcast(I32),
+                    in_=v_sc[first : first + 4, :].bitcast(I32),
                 )
 
         w4_codes = held([P, PASSES, 2 * H], U8, "w4_codes")
@@ -135,7 +118,7 @@ def tile_list_glove_pattern_chooser_kernel(
             count = raw.shape[2] // PACK
             copy(
                 grouped[:, :, first_m : first_m + count, :].rearrange("p t m j -> p m j t"),
-                raw[:].rearrange("p j (m t) -> p m j t", t=PACK),
+                raw.rearrange("p j (m t) -> p m j t", t=PACK),
             )
 
         def quantise(grouped, codes, scales, t0, t1):
@@ -151,7 +134,7 @@ def tile_list_glove_pattern_chooser_kernel(
         v_w, w1_q, w2_q = [], [], []
         for a in range(PASSES):
             grouped = held([P, PACK, P, PACK], BF16, "w1_bf%d" % a)
-            round_piece(nc.scalar.copy, grouped, w1_raw[a][0], 0)
+            round_piece(nc.scalar.copy, grouped, w1_raw[:, a, :, :], 0)
             w1_q.append(mx_tiles("w1_%d" % a, H))
             quantise(grouped, w1_q[a][0], w1_q[a][1], 0, PACK)
             v_w.append(held([P, S], U32, "v_w%d" % a))
@@ -160,6 +143,17 @@ def tile_list_glove_pattern_chooser_kernel(
                     v_w[a][:, hf * BANK : (hf + 1) * BANK],
                     tab_w[a][:].indirect(offs_sb[:, hf * 32 : (hf + 1) * 32]),
                 )
+        w2_rows = w2.rearrange("(a p j) c -> a p j c", p=P, j=PACK)
+        w2_first = staged([P, PACK, H], F32, "w2_first", 48)
+        nc.sync.dma_start(out=w2_first[:], in_=w2_rows[0])
+        w2_raw = [[w2_first[:, :, 0 : H // 2], w2_first[:, :, H // 2 : H]], []]
+        for i in range(2):
+            piece = staged([P, PACK, H // 2], F32, "w2_last%d" % i, 56 + 4 * i)
+            nc.sync.dma_start(out=piece[:], in_=w2_rows[1][:, :, i * H // 2 : (i + 1) * H // 2])
+            w2_raw[1].append(piece[:])
+        left_sb = staged([P, PACK, NP], F32, "left_sb", 16)
+        nc.sync.dma_start(out=left_sb[:], in_=left.rearrange("(p t) n -> p t n", t=PACK))
+        tab2_w = load_words(tab2_words, 0, T3, "tab2_w", 24)
         for a in range(PASSES):
             grouped = held([P, PACK, P, PACK], BF16, "w2_bf%d" % a)
             round_piece(nc.scalar.copy, grouped, w2_raw[a][0], 0)
@@ -167,6 +161,12 @@ def tile_list_glove_pattern_chooser_kernel(
             w2_q.append(mx_tiles("w2_%d" % a, H))
             quantise(grouped, w2_q[a][0], w2_q[a][1], 0, 1)
             quantise(grouped, w2_q[a][0], w2_q[a][1], 1, PACK)
+
+        fit_rows = fit.rearrange("(c p) n -> p c n", p=P)
+        fit_sb = []
+        for g, kib in enumerate((48, 56)):
+            fit_sb.append(staged([P, M_TILES // 2, NP], F32, "fit_sb%d" % g, kib))
+            nc.sync.dma_start(out=fit_sb[g][:], in_=fit_rows[:, 4 * g : 4 * g + 4, :])
 
         def product(kind, t, hf):
             cols = slice(hf * BANK, (hf + 1) * BANK)
@@ -192,13 +192,18 @@ def tile_list_glove_pattern_chooser_kernel(
         x2_bf = held([P, NP, PACK], BF16, "x2_bf", tag="w1_bf1")
         larger = {}
 
+        b1_sb = {}
+
+        def first_product(t):
+            for hf in range(HALVES):
+                b1 = product("b1", t, hf)
+                b1_sb[t, hf] = held([P, BANK], F32, "b1_sb%d_%d" % (t, hf))
+                nc.scalar.copy(b1_sb[t, hf][:], b1[:])
+
         def maximum(t, hf):
-            b1 = product("b1", t, hf)
-            b1_sb = held([P, BANK], F32, "b1_sb%d_%d" % (t, hf))
-            nc.scalar.copy(b1_sb[:], b1[:])
             b2 = product("b2", t, hf)
             larger[t, hf] = ring.tile([P, BANK], F32, name="larger")
-            nc.vector.tensor_tensor(larger[t, hf][:], b2[:], b1_sb[:], ALU.max)
+            nc.vector.tensor_tensor(larger[t, hf][:], b2[:], b1_sb[t, hf][:], ALU.max)
 
         def join(t, hf):
             b3 = product("b3", t, hf)
@@ -212,6 +217,7 @@ def tile_list_glove_pattern_chooser_kernel(
             nc.vector.tensor_tensor(g1[:], u[t][:].indirect(pos1_sb[:]), left_sb[:, t, :], ALU.mult)
             nc.scalar.activation(x1_bf[:, :, t], g1[:], ACT.Copy, scale=gain_sb[:, t : t + 1])
 
+        first_product(0)
         for t in range(PACK):
             maximum(t, 0)
             if t > 0:
@@ -219,8 +225,13 @@ def tile_list_glove_pattern_chooser_kernel(
             maximum(t, 1)
             join(t, 0)
             join(t, 1)
+            if t + 1 < PACK:
+                first_product(t + 1)
         pick(PACK - 1)
 
+        bias_sb = staged([P, M_TILES], F32, "bias_sb", 16)
+        with nc.allow_non_contiguous_dma(reason="one bias value a partition"):
+            nc.sync.dma_start(out=bias_sb[:], in_=bias.rearrange("(c p) -> p c", p=P))
         v2_w = held([P, S2], U32, "v2_w", tag="u%d" % (PACK - 1))
         x_q = {}
         for hf, (name, x_bf) in enumerate((("x2", x2_bf), ("x1", x1_bf))):
@@ -248,21 +259,24 @@ def tile_list_glove_pattern_chooser_kernel(
 
         def minimum(i):
             e2 = score("x2", "b3", i)
-            e2_sb = ring.tile([P, NP], F32, name="e2_sb")
+            e2_sb = held([P, NP], F32, "e2_sb%d" % i, tag="b1_sb%d_%d" % divmod(i, HALVES))
             nc.scalar.copy(e2_sb[:], e2[:])
             e1 = score("x1", "b2", i)
             smaller[i] = ring.tile([P, NP], F32, name="smaller")
             nc.vector.tensor_tensor(smaller[i][:], e1[:], e2_sb[:], ALU.min)
 
-        def finish(i):
-            fitted = ring.tile([P, NP], F32, name="fitted")
-            nc.vector.tensor_tensor(fitted[:], smaller[i][:], fit_sb[:, i, :], ALU.mult)
-            result = ring.tile([P, NP], F32, name="result")
-            nc.scalar.activation(result[:], fitted[:], ACT.Identity, bias=bias_sb[:, i : i + 1])
-            nc.sync.dma_start(out=out[i * P : (i + 1) * P, :], in_=result[:])
+        def finish(i, pieces=1):
+            width = NP // pieces
+            for c in range(pieces):
+                cols = slice(c * width, (c + 1) * width)
+                fitted = ring.tile([P, width], F32, name="fitted")
+                nc.vector.tensor_tensor(fitted[:], smaller[i][:, cols], fit_sb[i // 4][:, i % 4, cols], ALU.mult)
+                result = ring.tile([P, width], F32, name="result")
+                nc.scalar.activation(result[:], fitted[:], ACT.Identity, bias=bias_sb[:, i : i + 1])
+                nc.sync.dma_start(out=out[i * P : (i + 1) * P, cols], in_=result[:])
 
         for i in range(M_TILES):
             minimum(i)
             if i > 0:
                 finish(i - 1)
-        finish(M_TILES - 1)
+        finish(M_TILES - 1, pieces=2)

@@ -48,13 +48,14 @@ def tile_list_glove_pattern_chooser_kernel(
         tab_sc = held([P, T], U8, "tab_sc")
         tab2_sc = held([P, T3], U8, "tab2_sc")
         w4_sc_raw = held([P, PASSES, H], U8, "w4_sc_raw")
-        v_planes = [held([P, S], U8, "v_plane%d" % a) for a in range(PASSES)]
         v2_plane = held([P, S2], U8, "v2_plane")
 
+        v_planes = [held([P, S], U8, "v_plane%d" % a) for a in range(PASSES)]
+
         nc.gpsimd.memset(tab2_sc[:].bitcast(I32), 0)
+        nc.gpsimd.memset(w4_sc_raw[:].rearrange("p a c -> p (a c)").bitcast(I32), 0)
         nc.vector.memset(tab_sc[32:64, :].bitcast(I32), 0)
         nc.vector.memset(tab_sc[64:P, :].bitcast(I32), 0)
-        nc.vector.memset(w4_sc_raw[:].rearrange("p a c -> p (a c)").bitcast(I32), 0)
         for plane in v_planes + [v2_plane]:
             nc.gpsimd.memset(plane[:].bitcast(I32), 0)
 
@@ -64,43 +65,41 @@ def tile_list_glove_pattern_chooser_kernel(
             return tile
 
         nc.sync.dma_start(offs_sb[:], offs)
+        w4_raw = held([P, PASSES, 2 * H], U8, "w4_raw")
+        nc.sync.dma_start(out=w4_raw[:].bitcast(I32), in_=w4_words.rearrange("a p b -> p a b").bitcast(I32))
         nc.sync.dma_start(
             out=tab_sc[0:32, :].bitcast(I32),
             in_=tab_scales.rearrange("a q t -> (a q) t").bitcast(I32),
         )
         nc.sync.dma_start(offs2_sb[:], offs2)
-        nc.sync.dma_start(pos1_sb[:], pos1)
-        nc.sync.dma_start(pos2_sb[:], pos2)
-        w4_raw = held([P, PASSES, 2 * H], U8, "w4_raw")
-        nc.sync.dma_start(out=w4_raw[:].bitcast(I32), in_=w4_words.rearrange("a p b -> p a b").bitcast(I32))
         nc.sync.dma_start(out=tab2_sc[0:P:8, :].bitcast(I32), in_=tab2_scales[0].bitcast(I32))
         w1_raw = staged([P, PASSES, PACK, H], F32, "w1_raw", 32)
         nc.sync.dma_start(out=w1_raw[:], in_=w1.rearrange("(a p j) c -> p a j c", p=P, j=PACK))
+        tab_w = [load_words(tab_words, 0, T, "tab_w0", 0)]
         for q in range(4):
             nc.sync.dma_start(
                 out=w4_sc_raw[32 * q : 32 * q + 4, :, :].bitcast(I32),
                 in_=w4_scales[:, 4 * q : 4 * q + 4, :].rearrange("a r c -> r a c").bitcast(I32),
             )
-        tab_w = [load_words(tab_words, a, T, "tab_w%d" % a, 16 * a) for a in range(PASSES)]
-        gain_sb = held([P, PACK], F32, "gain_sb")
-        nc.sync.dma_start(out=gain_sb[:], in_=gain.rearrange("(p t) -> p t", t=PACK))
+        tab_w.append(load_words(tab_words, 1, T, "tab_w1", 16))
+
+        w4_codes = held([P, PASSES, 2 * H], U8, "w4_codes")
+        nc.vector.tensor_copy(
+            w4_codes[:].bitcast(U16).rearrange("p a (t m) -> p a m t", t=PACK),
+            w4_raw[:].bitcast(U16).rearrange("p a (m t) -> p a m t", t=PACK),
+        )
 
         v_sc = held([P, S], U8, "v_sc")
         nc.vector.tensor_copy(v_sc[:], tab_sc[:].indirect(offs_sb[:]))
         for a in range(PASSES):
             for q in range(4):
                 first = 16 * a + 4 * q
-                (nc.scalar if a == 0 else nc.gpsimd).dma_start(
+                nc.gpsimd.dma_start(
                     out=v_planes[a][32 * q : 32 * q + 4, :].bitcast(I32),
                     in_=v_sc[first : first + 4, :].bitcast(I32),
                 )
 
-        w4_codes = held([P, PASSES, 2 * H], U8, "w4_codes")
         w4_sc = held([P, PASSES, H], U8, "w4_sc")
-        nc.vector.tensor_copy(
-            w4_codes[:].bitcast(U16).rearrange("p a (t m) -> p a m t", t=PACK),
-            w4_raw[:].bitcast(U16).rearrange("p a (m t) -> p a m t", t=PACK),
-        )
         nc.vector.tensor_copy(
             w4_sc[:].rearrange("p a (t m) -> p a m t", t=PACK),
             w4_sc_raw[:].rearrange("p a (m t) -> p a m t", t=PACK),
@@ -151,9 +150,13 @@ def tile_list_glove_pattern_chooser_kernel(
             piece = staged([P, PACK, H // 2], F32, "w2_last%d" % i, 56 + 4 * i)
             nc.sync.dma_start(out=piece[:], in_=w2_rows[1][:, :, i * H // 2 : (i + 1) * H // 2])
             w2_raw[1].append(piece[:])
-        left_sb = staged([P, PACK, NP], F32, "left_sb", 16)
+        left_sb = staged([P, PACK, NP], F32, "left_sb", 32)
         nc.sync.dma_start(out=left_sb[:], in_=left.rearrange("(p t) n -> p t n", t=PACK))
-        tab2_w = load_words(tab2_words, 0, T3, "tab2_w", 24)
+        nc.sync.dma_start(pos1_sb[:], pos1)
+        nc.sync.dma_start(pos2_sb[:], pos2)
+        gain_sb = held([P, PACK], F32, "gain_sb")
+        nc.sync.dma_start(out=gain_sb[:], in_=gain.rearrange("(p t) -> p t", t=PACK))
+        tab2_w = load_words(tab2_words, 0, T3, "tab2_w", 0)
         for a in range(PASSES):
             grouped = held([P, PACK, P, PACK], BF16, "w2_bf%d" % a)
             round_piece(nc.scalar.copy, grouped, w2_raw[a][0], 0)
@@ -164,7 +167,7 @@ def tile_list_glove_pattern_chooser_kernel(
 
         fit_rows = fit.rearrange("(c p) n -> p c n", p=P)
         fit_sb = []
-        for g, kib in enumerate((48, 56)):
+        for g, kib in enumerate((16, 24)):
             fit_sb.append(staged([P, M_TILES // 2, NP], F32, "fit_sb%d" % g, kib))
             nc.sync.dma_start(out=fit_sb[g][:], in_=fit_rows[:, 4 * g : 4 * g + 4, :])
 
@@ -197,7 +200,11 @@ def tile_list_glove_pattern_chooser_kernel(
         def first_product(t):
             for hf in range(HALVES):
                 b1 = product("b1", t, hf)
-                b1_sb[t, hf] = held([P, BANK], F32, "b1_sb%d_%d" % (t, hf))
+                name = "b1_sb%d_%d" % (t, hf)
+                if t == 0:
+                    b1_sb[t, hf] = staged([P, BANK], F32, name, 56 + 2 * hf)
+                else:
+                    b1_sb[t, hf] = held([P, BANK], F32, name)
                 nc.scalar.copy(b1_sb[t, hf][:], b1[:])
 
         def maximum(t, hf):
@@ -229,7 +236,7 @@ def tile_list_glove_pattern_chooser_kernel(
                 first_product(t + 1)
         pick(PACK - 1)
 
-        bias_sb = staged([P, M_TILES], F32, "bias_sb", 16)
+        bias_sb = staged([P, M_TILES], F32, "bias_sb", 32)
         with nc.allow_non_contiguous_dma(reason="one bias value a partition"):
             nc.sync.dma_start(out=bias_sb[:], in_=bias.rearrange("(c p) -> p c", p=P))
         v2_w = held([P, S2], U32, "v2_w", tag="u%d" % (PACK - 1))
@@ -259,7 +266,7 @@ def tile_list_glove_pattern_chooser_kernel(
 
         def minimum(i):
             e2 = score("x2", "b3", i)
-            e2_sb = held([P, NP], F32, "e2_sb%d" % i, tag="b1_sb%d_%d" % divmod(i, HALVES))
+            e2_sb = held([P, NP], F32, "e2_sb%d" % i, )
             nc.scalar.copy(e2_sb[:], e2[:])
             e1 = score("x1", "b2", i)
             smaller[i] = ring.tile([P, NP], F32, name="smaller")
@@ -271,7 +278,7 @@ def tile_list_glove_pattern_chooser_kernel(
                 cols = slice(c * width, (c + 1) * width)
                 fitted = ring.tile([P, width], F32, name="fitted")
                 nc.vector.tensor_tensor(fitted[:], smaller[i][:, cols], fit_sb[i // 4][:, i % 4, cols], ALU.mult)
-                result = ring.tile([P, width], F32, name="result")
+                result = held([P, width], F32, "result%d_%d" % (i, c))
                 nc.scalar.activation(result[:], fitted[:], ACT.Identity, bias=bias_sb[:, i : i + 1])
                 nc.sync.dma_start(out=out[i * P : (i + 1) * P, cols], in_=result[:])
 

from contextlib import ExitStack

import concourse.mybir as mybir

K, T, S, H, S2, T3, NP = 1024, 4096, 1024, 512, 1024, 2048, 512
FLOPS = 2 * 3 * K * H * S + 2 * 2 * H * S2 * NP

F32 = mybir.dt.float32
BF16 = mybir.dt.bfloat16
I32 = mybir.dt.int32
U32 = mybir.dt.uint32
U16 = mybir.dt.uint16
U8 = mybir.dt.uint8
FP8X4 = mybir.dt.float8_e4m3fn_x4
FP4X4 = mybir.dt.float4_e2m1fn_x4
ALU = mybir.AluOpType
ACT = mybir.ActivationFunctionType

P = 128
PACK = 4
PASSES = K // (P * PACK)
BANK = 512
HALVES = S // BANK
M_TILES = S2 // P


def tile_list_glove_pattern_chooser_kernel(
    tc, tab_words, tab_scales, offs, tab2_words, tab2_scales, offs2, pos1, pos2,
    w1, w2, w4_words, w4_scales, gain, left, fit, bias, out,
):
    nc = tc.nc
    with ExitStack() as ctx:
        keep = ctx.enter_context(tc.tile_pool(name="keep", bufs=1))
        stage = ctx.enter_context(tc.tile_pool(name="stage", bufs=1))
        ring = ctx.enter_context(tc.tile_pool(name="ring", bufs=3))
        psum = ctx.enter_context(tc.psum_pool(name="psum", bufs=1))

        def held(shape, dtype, name, tag=None):
            return keep.tile(shape, dtype, name=name, tag=tag or name, align_bytes=64)

        def staged(shape, dtype, name, kib):
            return stage.tile(shape, dtype, name=name, offset=kib * 1024)

        offs_sb = held([P, S // 16], U16, "offs_sb")
        offs2_sb = held([P, S2 // 16], U16, "offs2_sb")
        pos1_sb = held([P, NP // 16], U16, "pos1_sb")
        pos2_sb = held([P, NP // 16], U16, "pos2_sb")
        tab_sc = held([P, T], U8, "tab_sc")
        tab2_sc = held([P, T3], U8, "tab2_sc")
        w4_sc_raw = held([P, PASSES, H], U8, "w4_sc_raw")
        v2_plane = held([P, S2], U8, "v2_plane")

        v_planes = [held([P, S], U8, "v_plane%d" % a) for a in range(PASSES)]

        nc.gpsimd.memset(tab2_sc[:].bitcast(I32), 0)
        nc.gpsimd.memset(w4_sc_raw[:].rearrange("p a c -> p (a c)").bitcast(I32), 0)
        nc.vector.memset(tab_sc[32:64, :].bitcast(I32), 0)
        nc.vector.memset(tab_sc[64:P, :].bitcast(I32), 0)
        for plane in v_planes + [v2_plane]:
            nc.gpsimd.memset(plane[:].bitcast(I32), 0)

        def load_words(words, a, width, name, kib):
            tile = staged([P, width], U32, name, kib)
            nc.sync.dma_start(out=tile[:].bitcast(I32), in_=words[a].rearrange("p t i -> p (t i)").bitcast(I32))
            return tile

        nc.sync.dma_start(offs_sb[:], offs)
        w4_raw = held([P, PASSES, 2 * H], U8, "w4_raw")
        nc.sync.dma_start(out=w4_raw[:].bitcast(I32), in_=w4_words.rearrange("a p b -> p a b").bitcast(I32))
        nc.sync.dma_start(
            out=tab_sc[0:32, :].bitcast(I32),
            in_=tab_scales.rearrange("a q t -> (a q) t").bitcast(I32),
        )
        nc.sync.dma_start(offs2_sb[:], offs2)
        nc.sync.dma_start(out=tab2_sc[0:P:8, :].bitcast(I32), in_=tab2_scales[0].bitcast(I32))
        w1_raw = staged([P, PASSES, PACK, H], F32, "w1_raw", 32)
        nc.sync.dma_start(out=w1_raw[:], in_=w1.rearrange("(a p j) c -> p a j c", p=P, j=PACK))
        tab_w = [load_words(tab_words, 0, T, "tab_w0", 0)]
        for q in range(4):
            nc.sync.dma_start(
                out=w4_sc_raw[32 * q : 32 * q + 4, :, :].bitcast(I32),
                in_=w4_scales[:, 4 * q : 4 * q + 4, :].rearrange("a r c -> r a c").bitcast(I32),
            )
        tab_w.append(load_words(tab_words, 1, T, "tab_w1", 16))

        w4_codes = held([P, PASSES, 2 * H], U8, "w4_codes")
        nc.vector.tensor_copy(
            w4_codes[:].bitcast(U16).rearrange("p a (t m) -> p a m t", t=PACK),
            w4_raw[:].bitcast(U16).rearrange("p a (m t) -> p a m t", t=PACK),
        )

        v_sc = held([P, S], U8, "v_sc")
        nc.vector.tensor_copy(v_sc[:], tab_sc[:].indirect(offs_sb[:]))
        for a in range(PASSES):
            for q in range(4):
                first = 16 * a + 4 * q
                nc.gpsimd.dma_start(
                    out=v_planes[a][32 * q : 32 * q + 4, :].bitcast(I32),
                    in_=v_sc[first : first + 4, :].bitcast(I32),
                )

        w4_sc = held([P, PASSES, H], U8, "w4_sc")
        nc.vector.tensor_copy(
            w4_sc[:].rearrange("p a (t m) -> p a m t", t=PACK),
            w4_sc_raw[:].rearrange("p a (m t) -> p a m t", t=PACK),
        )

        v2_sc = held([P, S2], U8, "v2_sc")
        nc.vector.tensor_copy(v2_sc[:], tab2_sc[:].indirect(offs2_sb[:]))
        for q in range(4):
            nc.gpsimd.dma_start(
                out=v2_plane[32 * q : 32 * q + 4, :].bitcast(I32),
                in_=v2_sc[32 * q : 32 * q + 32 : 8, :].bitcast(I32),
            )

        def round_piece(copy, grouped, raw, first_m):
            count = raw.shape[2] // PACK
            copy(
                grouped[:, :, first_m : first_m + count, :].rearrange("p t m j -> p m j t"),
                raw.rearrange("p j (m t) -> p m j t", t=PACK),
            )

        def quantise(grouped, codes, scales, t0, t1):
            nc.vector.quantize_mx(
                out=codes[:, t0 * P : t1 * P].bitcast(FP8X4),
                scales=scales[:, t0 * P : t1 * P],
                in_=grouped[:, t0:t1, :, :].rearrange("p t m j -> p (t m j)"),
            )

        def mx_tiles(name, width):
            return held([P, width], U32, name + "_codes"), held([P, width], U8, name + "_scales")

        v_w, w1_q, w2_q = [], [], []
        for a in range(PASSES):
            grouped = held([P, PACK, P, PACK], BF16, "w1_bf%d" % a)
            round_piece(nc.scalar.copy, grouped, w1_raw[:, a, :, :], 0)
            w1_q.append(mx_tiles("w1_%d" % a, H))
            quantise(grouped, w1_q[a][0], w1_q[a][1], 0, PACK)
            v_w.append(held([P, S], U32, "v_w%d" % a))
            for hf in range(HALVES):
                nc.vector.tensor_copy(
                    v_w[a][:, hf * BANK : (hf + 1) * BANK],
                    tab_w[a][:].indirect(offs_sb[:, hf * 32 : (hf + 1) * 32]),
                )
        w2_rows = w2.rearrange("(a p j) c -> a p j c", p=P, j=PACK)
        w2_first = staged([P, PACK, H], F32, "w2_first", 48)
        nc.sync.dma_start(out=w2_first[:], in_=w2_rows[0])
        w2_raw = [[w2_first[:, :, 0 : H // 2], w2_first[:, :, H // 2 : H]], []]
        for i in range(2):
            piece = staged([P, PACK, H // 2], F32, "w2_last%d" % i, 56 + 4 * i)
            nc.sync.dma_start(out=piece[:], in_=w2_rows[1][:, :, i * H // 2 : (i + 1) * H // 2])
            w2_raw[1].append(piece[:])
        left_sb = staged([P, PACK, NP], F32, "left_sb", 32)
        nc.sync.dma_start(out=left_sb[:], in_=left.rearrange("(p t) n -> p t n", t=PACK))
        nc.sync.dma_start(pos1_sb[:], pos1)
        nc.sync.dma_start(pos2_sb[:], pos2)
        gain_sb = held([P, PACK], F32, "gain_sb")
        nc.sync.dma_start(out=gain_sb[:], in_=gain.rearrange("(p t) -> p t", t=PACK))
        tab2_w = load_words(tab2_words, 0, T3, "tab2_w", 0)
        for a in range(PASSES):
            grouped = held([P, PACK, P, PACK], BF16, "w2_bf%d" % a)
            round_piece(nc.scalar.copy, grouped, w2_raw[a][0], 0)
            round_piece(nc.vector.tensor_copy, grouped, w2_raw[a][1], P // 2)
            w2_q.append(mx_tiles("w2_%d" % a, H))
            quantise(grouped, w2_q[a][0], w2_q[a][1], 0, 1)
            quantise(grouped, w2_q[a][0], w2_q[a][1], 1, PACK)

        fit_rows = fit.rearrange("(c p) n -> p c n", p=P)
        fit_sb = []
        for g, kib in enumerate((16, 24)):
            fit_sb.append(staged([P, M_TILES // 2, NP], F32, "fit_sb%d" % g, kib))
            nc.sync.dma_start(out=fit_sb[g][:], in_=fit_rows[:, 4 * g : 4 * g + 4, :])

        def product(kind, t, hf):
            cols = slice(hf * BANK, (hf + 1) * BANK)
            rows = slice(t * P, (t + 1) * P)
            acc = psum.tile([P, BANK], F32, name="acc_" + kind, tag=kind, bufs={"b1": 2, "b2": 3, "b3": 3}[kind])
            for a in range(PASSES):
                if kind == "b3":
                    lhs = w4_codes[:, a, 2 * t * P : 2 * (t + 1) * P].bitcast(FP4X4)
                    lhs_sc = w4_sc[:, a, rows]
                else:
                    codes, scales = (w1_q if kind == "b1" else w2_q)[a]
                    lhs = codes[:, rows].bitcast(FP8X4)
                    lhs_sc = scales[:, rows]
                nc.tensor.matmul_mx(
                    out=acc[:], lhsT=lhs, lhsT_scale=lhs_sc,
                    rhs=v_w[a][:, cols].bitcast(FP8X4), rhs_scale=v_planes[a][:, cols],
                    start=(a == 0), stop=(a == PASSES - 1),
                )
            return acc

        u = [held([P, S], F32, "u%d" % t) for t in range(PACK)]
        x1_bf = held([P, NP, PACK], BF16, "x1_bf", tag="w1_bf0")
        x2_bf = held([P, NP, PACK], BF16, "x2_bf", tag="w1_bf1")
        larger = {}

        b1_sb = {}

        def first_product(t):
            for hf in range(HALVES):
                b1 = product("b1", t, hf)
                name = "b1_sb%d_%d" % (t, hf)
                if t == 0:
                    b1_sb[t, hf] = staged([P, BANK], F32, name, 56 + 2 * hf)
                else:
                    b1_sb[t, hf] = held([P, BANK], F32, name)
                nc.scalar.copy(b1_sb[t, hf][:], b1[:])

        def maximum(t, hf):
            b2 = product("b2", t, hf)
            larger[t, hf] = ring.tile([P, BANK], F32, name="larger")
            nc.vector.tensor_tensor(larger[t, hf][:], b2[:], b1_sb[t, hf][:], ALU.max)

        def join(t, hf):
            b3 = product("b3", t, hf)
            nc.vector.tensor_tensor(u[t][:, hf * BANK : (hf + 1) * BANK], b3[:], larger[t, hf][:], ALU.add)

        def pick(t):
            g2 = ring.tile([P, NP], F32, name="g2")
            nc.vector.tensor_copy(g2[:], u[t][:].indirect(pos2_sb[:]))
            nc.scalar.activation(x2_bf[:, :, t], g2[:], ACT.Copy, scale=gain_sb[:, t : t + 1])
            g1 = ring.tile([P, NP], F32, name="g1")
            nc.vector.tensor_tensor(g1[:], u[t][:].indirect(pos1_sb[:]), left_sb[:, t, :], ALU.mult)
            nc.scalar.activation(x1_bf[:, :, t], g1[:], ACT.Copy, scale=gain_sb[:, t : t + 1])

        first_product(0)
        for t in range(PACK):
            maximum(t, 0)
            if t > 0:
                pick(t - 1)
            maximum(t, 1)
            join(t, 0)
            join(t, 1)
            if t + 1 < PACK:
                first_product(t + 1)
        pick(PACK - 1)

        bias_sb = staged([P, M_TILES], F32, "bias_sb", 32)
        with nc.allow_non_contiguous_dma(reason="one bias value a partition"):
            nc.sync.dma_start(out=bias_sb[:], in_=bias.rearrange("(c p) -> p c", p=P))
        v2_w = held([P, S2], U32, "v2_w", tag="u%d" % (PACK - 1))
        x_q = {}
        for hf, (name, x_bf) in enumerate((("x2", x2_bf), ("x1", x1_bf))):
            nc.vector.tensor_copy(
                v2_w[:, hf * BANK : (hf + 1) * BANK],
                tab2_w[:].indirect(offs2_sb[:, hf * 32 : (hf + 1) * 32]),
            )
            x_q[name] = mx_tiles(name, NP)
            nc.vector.quantize_mx(
                out=x_q[name][0][:].bitcast(FP8X4), scales=x_q[name][1][:],
                in_=x_bf[:].rearrange("p n t -> p (n t)"),
            )

        def score(name, tag, i):
            rows = slice(i * P, (i + 1) * P)
            acc = psum.tile([P, NP], F32, name="e_" + name, tag=tag, bufs=3)
            nc.tensor.matmul_mx(
                out=acc[:], lhsT=v2_w[:, rows].bitcast(FP8X4), lhsT_scale=v2_plane[:, rows],
                rhs=x_q[name][0][:].bitcast(FP8X4), rhs_scale=x_q[name][1][:],
                start=True, stop=True,
            )
            return acc

        smaller = {}

        def minimum(i):
            e2 = score("x2", "b3", i)
            e2_sb = held([P, NP], F32, "e2_sb%d" % i, )
            nc.scalar.copy(e2_sb[:], e2[:])
            e1 = score("x1", "b2", i)
            smaller[i] = ring.tile([P, NP], F32, name="smaller")
            nc.vector.tensor_tensor(smaller[i][:], e1[:], e2_sb[:], ALU.min)

        def finish(i, pieces=1):
            width = NP // pieces
            for c in range(pieces):
                cols = slice(c * width, (c + 1) * width)
                fitted = ring.tile([P, width], F32, name="fitted")
                nc.vector.tensor_tensor(fitted[:], smaller[i][:, cols], fit_sb[i // 4][:, i % 4, cols], ALU.mult)
                result = held([P, width], F32, "result%d_%d" % (i, c))
                nc.scalar.activation(result[:], fitted[:], ACT.Identity, bias=bias_sb[:, i : i + 1])
                nc.sync.dma_start(out=out[i * P : (i + 1) * P, cols], in_=result[:])

        for i in range(M_TILES):
            minimum(i)
            if i > 0:
                finish(i - 1)
        finish(M_TILES - 1, pieces=2)
